import numpy as np
import ml_dtypes


def mxq(x, axis, fmt="e4m3"):
    dtype, down = {"e4m3": (ml_dtypes.float8_e4m3fn, 7), "e5m2": (ml_dtypes.float8_e5m2, 14)}[fmt]
    v = np.moveaxis(np.asarray(x, np.float32).astype(ml_dtypes.bfloat16).astype(np.float64), axis, -1)
    blocks = v.reshape(v.shape[:-1] + (-1, 32))
    amax = np.abs(blocks).max(-1, keepdims=True)
    byte = np.maximum(np.where(amax > 0, np.frexp(amax)[1] - 1 + 127, 0) - down, 1)
    scale = np.exp2(byte - 127.0)
    codes = (blocks / scale).astype(np.float32).astype(dtype).astype(np.float64)
    return np.moveaxis((codes * scale).reshape(v.shape), -1, axis)


WIDE = False


def mx_kscale(k):
    if not WIDE:
        return np.ones(k)
    levels = np.array([10, -10, 5, -5, 0])
    if k % 512:
        return np.exp2(np.random.permutation(np.resize(levels, k // 32))).repeat(32)
    a = np.empty((k // 512, 16))
    for p in range(k // 512):
        a[p, :8] = np.random.permutation(np.resize(levels, 8))
        for g in range(8):
            far = levels[np.abs(levels - a[p, g]) >= 10]
            a[p, g + 8] = far[np.random.randint(len(far))]
    return np.exp2(a.ravel()).repeat(32)


def f64(x):
    return np.asarray(x).astype(np.float64)


def striped(idx):
    return np.tile(idx.reshape(-1, 16).T, (8, 1)).astype(np.uint16)


def unstriped(offs):
    return offs[:16].T.reshape(-1).astype(np.int64)


def striped8(idx):
    return np.concatenate([x.reshape(-1, 16).T for x in idx]).astype(np.uint16)


def runs(offs, k):
    lists = np.stack([offs[16 * r : 16 * r + 16].T.reshape(-1) for r in range(8)]).astype(np.int64)
    return lists[np.arange(k) % 512 // 64]


def pack_weight(w):
    k, n = w.shape
    w = f64(np.asarray(w, np.float32).astype(ml_dtypes.bfloat16)).reshape(k // 32, 32, n)
    amax = np.abs(w).max(1)
    byte = np.clip(np.where(amax > 0, np.frexp(amax)[1] - 1 + 127 - 7, 1), 1, 254)
    scaled = (w * np.exp2(127.0 - byte)[:, None, :]).reshape(k, n).astype(np.float32)
    words = np.ascontiguousarray(scaled.reshape(k // 512, 128, 4, n).transpose(0, 1, 3, 2)).astype(ml_dtypes.float8_e4m3fn).view(np.uint8)
    return words, np.ascontiguousarray(byte.astype(np.uint8).reshape(k // 512, 16, n))


def unpack_weight(words, scales):
    g, p, n, _ = words.shape
    vals = np.ascontiguousarray(words).view(ml_dtypes.float8_e4m3fn).astype(np.float64) * np.repeat(np.exp2(scales.astype(np.float64) - 127.0), 8, axis=1)[..., None]
    return vals.transpose(0, 1, 3, 2).reshape(g * 512, n)


E2M1 = np.array([0.0, 0.5, 1.0, 1.5, 2.0, 3.0, 4.0, 6.0, -0.0, -0.5, -1.0, -1.5, -2.0, -3.0, -4.0, -6.0])


def pack_fp4(w):
    k, n = w.shape
    w = f64(np.asarray(w, np.float32).astype(ml_dtypes.bfloat16)).reshape(k // 32, 32, n)
    amax = np.abs(w).max(1)
    mant, ex = np.frexp(amax / 6.0)
    byte = np.clip(np.where(amax > 0, np.where(mant > 0.5, ex, ex - 1) + 127, 1), 1, 254)
    scaled = (w * np.exp2(127.0 - byte)[:, None, :]).reshape(k, n).astype(np.float32)
    c = np.ascontiguousarray(scaled.reshape(k // 512, 128, 4, n).transpose(0, 1, 3, 2)).astype(ml_dtypes.float4_e2m1fn).view(np.uint8) & 0xF
    words = (c[..., 0::2] | (c[..., 1::2] << 4)).reshape(k // 512, 128, 2 * n)
    return np.ascontiguousarray(words), np.ascontiguousarray(byte.astype(np.uint8).reshape(k // 512, 16, n))


def unpack_fp4(words, scales):
    g, _, n = scales.shape
    words = np.ascontiguousarray(words).reshape(g, 128, n, 2)
    nib = np.empty((g, 128, n, 4), np.uint8)
    nib[..., 0::2] = words & 0xF
    nib[..., 1::2] = words >> 4
    vals = E2M1[nib] * np.repeat(np.exp2(scales.astype(np.float64) - 127.0), 8, axis=1)[..., None]
    return vals.transpose(0, 1, 3, 2).reshape(g * 512, n)


def sigmoid(v):
    return 1.0 / (1.0 + np.exp(-np.maximum(v, -700.0)))

def planes(y):
    n, m = y.shape
    v = y.astype(np.float32).astype(ml_dtypes.bfloat16).astype(np.float64).reshape(n // 32, 32, m)
    top = np.abs(v).max(1)
    byte = np.clip(np.where(top > 0, np.frexp(top)[1] - 1 + 127 - 7, 1), 1, 254)
    codes = (v * np.exp2(127.0 - byte)[:, None, :]).reshape(n, m).astype(np.float32).astype(ml_dtypes.float8_e4m3fn).view(np.uint8)
    words = codes.reshape(n // 512, 128, 4, m).transpose(0, 1, 3, 2)
    return np.ascontiguousarray(words), np.ascontiguousarray(byte.astype(np.uint8).reshape(n // 512, 16, m))


K, T, S, N, H = 512, 2048, 512, 512, 512


def setup_inputs():
    n = np.random.standard_normal
    s = mx_kscale(K)[:, None]
    u = mx_kscale(S)
    packed_xT = pack_weight(n((K, T)) * s)
    packed_w1 = pack_fp4(n((S, N)) / np.sqrt(S) / u[:, None])
    return {
        "x_words": packed_xT[0],
        "x_scales": packed_xT[1],
        "wa": (n((K, H)) / np.sqrt(K) / s).astype(np.float32),
        "gt": (np.random.uniform(0.5, 1.5, (S, 1)) * u[:, None]).astype(np.float32),
        "w1_words": packed_w1[0],
        "w1_scales": packed_w1[1],
        "offs": striped(np.random.permutation(T)[:S]),
        "n1": striped8(np.stack([np.random.permutation(H) for _ in range(8)])),
        "n2": striped8(np.stack([np.random.permutation(H) for _ in range(8)])),
        "n3": striped8(np.stack([np.random.permutation(H) for _ in range(8)])),
        "n4": striped8(np.stack([np.random.permutation(H) for _ in range(8)])),
    }


def reference(x_words, x_scales, wa, gt, w1_words, w1_scales, offs, n1, n2, n3, n4):
    xq = unpack_weight(x_words, x_scales)[:, unstriped(offs)]
    y = xq.T @ mxq(f64(wa), 0, "e4m3")
    sm = np.maximum(y, y[np.arange(S)[:, None], runs(n2, S)])
    ds = np.zeros((S, H))
    ds[np.arange(S)[:, None], runs(n1, S)] = sm
    z = f64(gt) * (ds * sigmoid(y))
    h = unpack_fp4(w1_words, w1_scales).T @ mxq(z, 0, "e4m3")
    out_0 = h[np.arange(N)[:, None], runs(n3, N)] - (h[np.arange(N)[:, None], runs(n4, N)])
    return (out_0,) + planes(out_0)

@@ -1,0 +1,227 @@
+from contextlib import ExitStack
+
+import concourse.mybir as mybir
+
+K, T, S, N, H = 512, 2048, 512, 512, 512
+FLOPS = 2 * K * S * H + 2 * S * N * H
+
+F32 = mybir.dt.float32
+BF16 = mybir.dt.bfloat16
+I32 = mybir.dt.int32
+U32 = mybir.dt.uint32
+U16 = mybir.dt.uint16
+U8 = mybir.dt.uint8
+FP8X4 = mybir.dt.float8_e4m3fn_x4
+FP4X4 = mybir.dt.float4_e2m1fn_x4
+ALU = mybir.AluOpType
+ACT = mybir.ActivationFunctionType
+
+P = 128
+PACK = 4
+LIST = 16
+HALF = H // 2
+WA_PIECES = [(0, 256), (256, 384), (384, 512)]
+HALVES = [(0, HALF), (HALF, H)]
+
+
+def interleave(engine_copy, dst, src):
+    engine_copy(
+        out=dst.rearrange("p (c i) t -> p c t i", i=4),
+        in_=src.rearrange("p t (c i) -> p c t i", i=4),
+    )
+
+
+def tile_picked_toksendggap_none_po_kernel(
+    tc, x_words, x_scales, wa, gt, w1_words, w1_scales, offs, n1, n2, n3, n4, out_0, out_1, out_2
+):
+    nc = tc.nc
+    with ExitStack() as ctx:
+        sb = ctx.enter_context(tc.tile_pool(name="sb", bufs=1))
+        ps = ctx.enter_context(tc.psum_pool(name="ps", bufs=1))
+
+        def tile(shape, dtype, name):
+            return sb.tile(shape, dtype, name=name, align_bytes=64)
+
+        def load_list(src, name):
+            dst = tile([P, H // LIST], U16, name)
+            nc.sync.dma_start(dst[:], src)
+            return dst
+
+        def load_scale_rows(queue, dst, src):
+            for q in range(4):
+                queue.dma_start(dst[32 * q : 32 * q + 4, :].bitcast(I32), src[0, 4 * q : 4 * q + 4, :].bitcast(I32))
+
+        xs = tile([P, T], U8, "xs")
+        w1s = tile([P, N], U8, "w1s")
+        nc.vector.memset(xs[:].bitcast(I32), 0)
+        nc.vector.memset(w1s[:].bitcast(I32), 0)
+        warm = tile([P, 2], F32, "warm")
+        nc.vector.memset(warm[:, 0:1], 0.0)
+
+        offs_t = load_list(offs, "offs_t")
+        xw = tile([P, T], I32, "xw")
+        nc.sync.dma_start(xw[:], x_words[0].rearrange("p n t -> p (n t)").bitcast(I32))
+        w1w = tile([P, 2 * N], U8, "w1w")
+        nc.scalar.dma_start(w1w[:].bitcast(I32), w1_words[0].bitcast(I32))
+        load_scale_rows(nc.scalar, xs, x_scales)
+        nc.scalar.activation(warm[:, 1:2], warm[:, 0:1], ACT.Sigmoid)
+        wa_rows = wa.rearrange("(p j) c -> p j c", j=PACK)
+        wa_raw = []
+        for i, (a, b) in enumerate(WA_PIECES):
+            raw = tile([P, PACK, b - a], F32, "wa_raw%d" % i)
+            nc.sync.dma_start(raw[:], wa_rows[:, :, a:b])
+            wa_raw.append(raw)
+        n2_t = load_list(n2, "n2_t")
+        load_scale_rows(nc.sync, w1s, w1_scales)
+        gt_t = tile([P, PACK], F32, "gt_t")
+        nc.sync.dma_start(gt_t[:], gt.rearrange("(p t) o -> p (t o)", t=PACK))
+        n1_t = load_list(n1, "n1_t")
+        n4_t = load_list(n4, "n4_t")
+        n3_t = load_list(n3, "n3_t")
+
+        w1w_d = tile([P, 2 * N], U8, "w1w_d")
+        nc.vector.tensor_copy(
+            w1w_d[:].rearrange("p (t m b) -> p t m b", t=PACK, b=2),
+            w1w[:].rearrange("p (m t b) -> p t m b", t=PACK, b=2),
+        )
+
+        xs_g = tile([P, S], U8, "xs_g")
+        nc.vector.tensor_copy(xs_g[:], xs[:].indirect(offs_t[:]))
+        xs_d = tile([P, S], U8, "xs_d")
+        nc.vector.tensor_copy(
+            xs_d[:].rearrange("p (t m) -> p t m", t=PACK), xs_g[:].rearrange("p (m t) -> p t m", t=PACK)
+        )
+        xw_d = tile([P, S], U32, "xw_d")
+        nc.vector.tensor_copy(
+            xw_d[:].rearrange("p (t m) -> p m t", t=PACK), xw[:].bitcast(U32).indirect(offs_t[:])
+        )
+
+        wa_q = tile([P, H], U32, "wa_q")
+        wa_s = tile([P, H], U8, "wa_s")
+        y = [tile([P, H], F32, "y%d" % t) for t in range(PACK)]
+
+        def product_1(t, a, b, name):
+            acc = ps.tile([P, b - a], F32, name=name)
+            m = slice(t * P, (t + 1) * P)
+            nc.tensor.matmul_mx(
+                out=acc[:],
+                lhsT=xw_d[:, m].bitcast(FP8X4),
+                lhsT_scale=xs_d[:, m],
+                rhs=wa_q[:, a:b].bitcast(FP8X4),
+                rhs_scale=wa_s[:, a:b],
+                start=True,
+                stop=True,
+            )
+            nc.scalar.copy(y[t][:, a:b], acc[:])
+
+        for i, (a, b) in enumerate(WA_PIECES):
+            grouped = tile([P, b - a, PACK], BF16, "wa_g%d" % i)
+            last = i == len(WA_PIECES) - 1
+            interleave(nc.vector.tensor_copy if last else nc.scalar.copy, grouped[:], wa_raw[i][:])
+            nc.vector.quantize_mx(
+                out=wa_q[:, a:b].bitcast(FP8X4), scales=wa_s[:, a:b], in_=grouped[:].rearrange("p c t -> p (c t)")
+            )
+        for i, (a, b) in enumerate(WA_PIECES):
+            product_1(0, a, b, "piece%d" % i)
+        for t in range(1, PACK):
+            product_1(t, 0, H, "bank%d" % t)
+
+        w1s_d = tile([P, N], U8, "w1s_d")
+        nc.vector.tensor_copy(
+            w1s_d[:].rearrange("p (t m) -> p t m", t=PACK), w1s[:].rearrange("p (m t) -> p t m", t=PACK)
+        )
+
+        sig = [tile([P, H], F32, "sig%d" % t) for t in range(PACK)]
+        for t in range(PACK):
+            nc.scalar.activation(sig[t][:], y[t][:], ACT.Sigmoid)
+
+        fetched = [tile([P, H], F32, "fetched%d" % t) for t in range(PACK)]
+        sm = [tile([P, H], F32, "sm%d" % t) for t in range(PACK)]
+        ds = [tile([P, 2 * H], F32, "ds%d" % t) for t in range(PACK)]
+        z_rows = tile([P, PACK - 1, H], BF16, "z_rows")
+        z_g = tile([P, H, PACK], BF16, "z_g")
+
+        def fetch(t):
+            for a, b in HALVES:
+                nc.vector.tensor_copy(fetched[t][:, a:b], y[t][:].indirect(n2_t[:, a // LIST : b // LIST]))
+
+        def larger(t):
+            nc.vector.tensor_tensor(sm[t][:], y[t][:], fetched[t][:], ALU.max)
+
+        def send(t):
+            nc.vector.tensor_copy(ds[t][:].indirect(n1_t[:]), sm[t][:])
+
+        def weigh(t, dst, a, b):
+            nc.vector.scalar_tensor_tensor(dst, ds[t][:, a:b], gt_t[:, t : t + 1], sig[t][:, a:b], ALU.mult, ALU.mult)
+
+        fetch(0)
+        fetch(1)
+        larger(0)
+        fetch(2)
+        larger(1)
+        fetch(3)
+        larger(2)
+        send(0)
+        larger(3)
+        send(1)
+        weigh(0, z_rows[:, 0, :], 0, H)
+        send(2)
+        weigh(1, z_rows[:, 1, :], 0, H)
+        nc.scalar.copy(z_g[:, :, 0:2], z_rows[:, 0:2, :].rearrange("p t c -> p c t"))
+        weigh(2, z_rows[:, 2, :], 0, H)
+        nc.scalar.copy(z_g[:, :, 2:4], z_rows[:, 2, :].unsqueeze(2).to_broadcast([P, H, 2]))
+        send(3)
+        for a, b in HALVES:
+            weigh(3, z_g[:, a:b, 3], a, b)
+
+        z_q = tile([P, H], U32, "z_q")
+        z_s = tile([P, H], U8, "z_s")
+        h = [tile([P, H], F32, "h%d" % t) for t in range(PACK)]
+
+        def product_2(t, a, b, name):
+            acc = ps.tile([P, b - a], F32, name=name)
+            nc.tensor.matmul_mx(
+                out=acc[:],
+                lhsT=w1w_d[:, 2 * t * P : 2 * (t + 1) * P].bitcast(FP4X4),
+                lhsT_scale=w1s_d[:, t * P : (t + 1) * P],
+                rhs=z_q[:, a:b].bitcast(FP8X4),
+                rhs_scale=z_s[:, a:b],
+                start=True,
+                stop=True,
+            )
+            nc.scalar.copy(h[t][:, a:b], acc[:])
+
+        for a, b in HALVES:
+            nc.vector.quantize_mx(
+                out=z_q[:, a:b].bitcast(FP8X4), scales=z_s[:, a:b], in_=z_g[:, a:b, :].rearrange("p c t -> p (c t)")
+            )
+        for i, (a, b) in enumerate(HALVES):
+            product_2(0, a, b, "piece%d" % i)
+        for t in range(1, PACK):
+            product_2(t, 0, H, "bank%d" % t)
+
+        out_rows = out_0.rearrange("(p t) c -> p t c", t=PACK)
+        out_words = out_1[0].rearrange("p n t -> p (n t)").bitcast(I32)
+        o_q = tile([P, H], I32, "o_q")
+        o_s = tile([P, H], U8, "o_s")
+        for i, (a, b) in enumerate(HALVES):
+            cols = slice(a // LIST, b // LIST)
+            res = tile([P, PACK, b - a], F32, "res%d" % i)
+            less = tile([P, PACK, b - a], F32, "less%d" % i)
+            for step in range(PACK + 1):
+                if step < PACK:
+                    nc.vector.tensor_copy(less[:, step, :], h[step][:].indirect(n4_t[:, cols]))
+                if step > 0:
+                    t = step - 1
+                    nc.vector.tensor_tensor(res[:, t, :], h[t][:].indirect(n3_t[:, cols]), less[:, t, :], ALU.subtract)
+                    nc.sync.dma_start(out_rows[:, t, a:b], res[:, t, :])
+            grouped = tile([P, b - a, PACK], BF16, "o_g%d" % i)
+            last = i == len(HALVES) - 1
+            interleave(nc.vector.tensor_copy if last else nc.scalar.copy, grouped[:], res[:])
+            nc.vector.quantize_mx(
+                out=o_q[:, a:b].bitcast(FP8X4), scales=o_s[:, a:b], in_=grouped[:].rearrange("p c t -> p (c t)")
+            )
+            nc.scalar.dma_start(out_words[:, a:b], o_q[:, a:b])
+        for q in range(4):
+            queue = nc.sync if q % 2 == 0 else nc.scalar
+            queue.dma_start(out_2[0, 4 * q : 4 * q + 4, :].bitcast(I32), o_s[32 * q : 32 * q + 4, :].bitcast(I32))

@@ -22,6 +22,7 @@ LIST = 16
 HALF = H // 2
 WA_PIECES = [(0, 256), (256, 384), (384, 512)]
 HALVES = [(0, HALF), (HALF, H)]
+LAST_ON_VECTOR = 160
 
 
 def interleave(engine_copy, dst, src):
@@ -53,58 +54,61 @@ def tile_picked_toksendggap_none_po_kernel(
 
         xs = tile([P, T], U8, "xs")
         w1s = tile([P, N], U8, "w1s")
-        nc.vector.memset(xs[:].bitcast(I32), 0)
-        nc.vector.memset(w1s[:].bitcast(I32), 0)
+        nc.gpsimd.memset(xs[:].bitcast(I32), 0)
         warm = tile([P, 2], F32, "warm")
         nc.vector.memset(warm[:, 0:1], 0.0)
+        nc.vector.memset(w1s[:].bitcast(I32), 0)
 
-        offs_t = load_list(offs, "offs_t")
-        xw = tile([P, T], I32, "xw")
-        nc.sync.dma_start(xw[:], x_words[0].rearrange("p n t -> p (n t)").bitcast(I32))
-        w1w = tile([P, 2 * N], U8, "w1w")
-        nc.scalar.dma_start(w1w[:].bitcast(I32), w1_words[0].bitcast(I32))
-        load_scale_rows(nc.scalar, xs, x_scales)
-        nc.scalar.activation(warm[:, 1:2], warm[:, 0:1], ACT.Sigmoid)
         wa_rows = wa.rearrange("(p j) c -> p j c", j=PACK)
-        wa_raw = []
-        for i, (a, b) in enumerate(WA_PIECES):
+
+        def load_wa(i):
+            a, b = WA_PIECES[i]
             raw = tile([P, PACK, b - a], F32, "wa_raw%d" % i)
             nc.sync.dma_start(raw[:], wa_rows[:, :, a:b])
-            wa_raw.append(raw)
+            return raw
+
+        load_scale_rows(nc.gpsimd, xs, x_scales)
+        xw = tile([P, T], I32, "xw")
+        nc.sync.dma_start(xw[:], x_words[0].rearrange("p n t -> p (n t)").bitcast(I32))
+        offs_t = load_list(offs, "offs_t")
+        nc.scalar.activation(warm[:, 1:2], warm[:, 0:1], ACT.Sigmoid)
+        wa_raw = [load_wa(i) for i in range(len(WA_PIECES))]
         n2_t = load_list(n2, "n2_t")
-        load_scale_rows(nc.sync, w1s, w1_scales)
         gt_t = tile([P, PACK], F32, "gt_t")
         nc.sync.dma_start(gt_t[:], gt.rearrange("(p t) o -> p (t o)", t=PACK))
         n1_t = load_list(n1, "n1_t")
+        w1w = tile([P, 2 * N], U8, "w1w")
+        nc.sync.dma_start(w1w[:].bitcast(I32), w1_words[0].bitcast(I32))
+        load_scale_rows(nc.sync, w1s, w1_scales)
         n4_t = load_list(n4, "n4_t")
         n3_t = load_list(n3, "n3_t")
 
-        w1w_d = tile([P, 2 * N], U8, "w1w_d")
-        nc.vector.tensor_copy(
-            w1w_d[:].rearrange("p (t m b) -> p t m b", t=PACK, b=2),
-            w1w[:].rearrange("p (m t b) -> p t m b", t=PACK, b=2),
-        )
-
-        xs_g = tile([P, S], U8, "xs_g")
-        nc.vector.tensor_copy(xs_g[:], xs[:].indirect(offs_t[:]))
-        xs_d = tile([P, S], U8, "xs_d")
-        nc.vector.tensor_copy(
-            xs_d[:].rearrange("p (t m) -> p t m", t=PACK), xs_g[:].rearrange("p (m t) -> p t m", t=PACK)
-        )
         xw_d = tile([P, S], U32, "xw_d")
         nc.vector.tensor_copy(
             xw_d[:].rearrange("p (t m) -> p m t", t=PACK), xw[:].bitcast(U32).indirect(offs_t[:])
         )
+        xs_g = tile([P, S], U8, "xs_g")
+        nc.vector.tensor_copy(xs_g[:], xs[:].indirect(offs_t[:]))
+        xs_d = tile([P, S], U8, "xs_d")
+
+        def deal_scales(t0, t1):
+            nc.vector.tensor_copy(
+                xs_d[:].rearrange("p (t m) -> p t m", t=PACK)[:, t0:t1, :],
+                xs_g[:].rearrange("p (m t) -> p t m", t=PACK)[:, t0:t1, :],
+            )
+
+        deal_scales(0, 1)
 
         wa_q = tile([P, H], U32, "wa_q")
         wa_s = tile([P, H], U8, "wa_s")
         y = [tile([P, H], F32, "y%d" % t) for t in range(PACK)]
 
-        def product_1(t, a, b, name):
-            acc = ps.tile([P, b - a], F32, name=name)
+        y_bank = [ps.tile([P, H], F32, name="y_bank%d" % t) for t in range(PACK)]
+
+        def product_1(t, a, b):
             m = slice(t * P, (t + 1) * P)
             nc.tensor.matmul_mx(
-                out=acc[:],
+                out=y_bank[t][:, a:b],
                 lhsT=xw_d[:, m].bitcast(FP8X4),
                 lhsT_scale=xs_d[:, m],
                 rhs=wa_q[:, a:b].bitcast(FP8X4),
@@ -112,28 +116,39 @@ def tile_picked_toksendggap_none_po_kernel(
                 start=True,
                 stop=True,
             )
-            nc.scalar.copy(y[t][:, a:b], acc[:])
+            nc.scalar.copy(y[t][:, a:b], y_bank[t][:, a:b])
 
+        wa_g = [tile([P, HALF, PACK], BF16, "wa_g%d" % i) for i in range(2)]
         for i, (a, b) in enumerate(WA_PIECES):
-            grouped = tile([P, b - a, PACK], BF16, "wa_g%d" % i)
             last = i == len(WA_PIECES) - 1
-            interleave(nc.vector.tensor_copy if last else nc.scalar.copy, grouped[:], wa_raw[i][:])
+            dst = wa_g[a // HALF][:, a % HALF : a % HALF + b - a, :]
+            interleave(nc.vector.tensor_copy if last else nc.scalar.copy, dst, wa_raw[i][:])
+        for i, (a, b) in enumerate(HALVES):
             nc.vector.quantize_mx(
-                out=wa_q[:, a:b].bitcast(FP8X4), scales=wa_s[:, a:b], in_=grouped[:].rearrange("p c t -> p (c t)")
+                out=wa_q[:, a:b].bitcast(FP8X4), scales=wa_s[:, a:b], in_=wa_g[i][:].rearrange("p c t -> p (c t)")
             )
-        for i, (a, b) in enumerate(WA_PIECES):
-            product_1(0, a, b, "piece%d" % i)
+        deal_scales(1, PACK)
+        for a, b in HALVES:
+            product_1(0, a, b)
         for t in range(1, PACK):
-            product_1(t, 0, H, "bank%d" % t)
+            product_1(t, 0, H)
 
-        w1s_d = tile([P, N], U8, "w1s_d")
-        nc.vector.tensor_copy(
+        w1w_d = tile([P, 2 * N], U8, "wa_g1")
+        nc.gpsimd.tensor_copy(
+            w1w_d[:].rearrange("p (t m b) -> p t m b", t=PACK, b=2),
+            w1w[:].rearrange("p (m t b) -> p t m b", t=PACK, b=2),
+        )
+        w1s_d = tile([P, N], U8, "wa_g0")
+        nc.gpsimd.tensor_copy(
             w1s_d[:].rearrange("p (t m) -> p t m", t=PACK), w1s[:].rearrange("p (m t) -> p t m", t=PACK)
         )
 
         sig = [tile([P, H], F32, "sig%d" % t) for t in range(PACK)]
+        gate = [tile([P, H], F32, "gate%d" % t) for t in range(PACK - 1)]
         for t in range(PACK):
             nc.scalar.activation(sig[t][:], y[t][:], ACT.Sigmoid)
+            if t < PACK - 1:
+                nc.scalar.activation(gate[t][:], sig[t][:], ACT.Copy, scale=gt_t[:, t : t + 1])
 
         fetched = [tile([P, H], F32, "fetched%d" % t) for t in range(PACK)]
         sm = [tile([P, H], F32, "sm%d" % t) for t in range(PACK)]
@@ -146,13 +161,16 @@ def tile_picked_toksendggap_none_po_kernel(
                 nc.vector.tensor_copy(fetched[t][:, a:b], y[t][:].indirect(n2_t[:, a // LIST : b // LIST]))
 
         def larger(t):
-            nc.vector.tensor_tensor(sm[t][:], y[t][:], fetched[t][:], ALU.max)
+            nc.vector.tensor_tensor(sm[t][:], y_bank[t][:], fetched[t][:], ALU.max)
 
         def send(t):
             nc.vector.tensor_copy(ds[t][:].indirect(n1_t[:]), sm[t][:])
 
         def weigh(t, dst, a, b):
             nc.vector.scalar_tensor_tensor(dst, ds[t][:, a:b], gt_t[:, t : t + 1], sig[t][:, a:b], ALU.mult, ALU.mult)
+
+        def weigh_aside(t, a, b):
+            nc.gpsimd.tensor_tensor(z_rows[:, t, a:b], ds[t][:, a:b], gate[t][:, a:b], ALU.mult)
 
         fetch(0)
         fetch(1)
@@ -162,14 +180,15 @@ def tile_picked_toksendggap_none_po_kernel(
         fetch(3)
         larger(2)
         send(0)
+        weigh_aside(0, 0, H)
         larger(3)
         send(1)
-        weigh(0, z_rows[:, 0, :], 0, H)
-        send(2)
-        weigh(1, z_rows[:, 1, :], 0, H)
+        weigh_aside(1, 0, H)
         nc.scalar.copy(z_g[:, :, 0:2], z_rows[:, 0:2, :].rearrange("p t c -> p c t"))
-        weigh(2, z_rows[:, 2, :], 0, H)
-        nc.scalar.copy(z_g[:, :, 2:4], z_rows[:, 2, :].unsqueeze(2).to_broadcast([P, H, 2]))
+        send(2)
+        for a, b in HALVES:
+            weigh_aside(2, a, b)
+            nc.scalar.copy(z_g[:, a:b, 2:4], z_rows[:, 2, a:b].unsqueeze(2).to_broadcast([P, b - a, 2]))
         send(3)
         for a, b in HALVES:
             weigh(3, z_g[:, a:b, 3], a, b)
@@ -196,9 +215,9 @@ def tile_picked_toksendggap_none_po_kernel(
                 out=z_q[:, a:b].bitcast(FP8X4), scales=z_s[:, a:b], in_=z_g[:, a:b, :].rearrange("p c t -> p (c t)")
             )
         for i, (a, b) in enumerate(HALVES):
-            product_2(0, a, b, "piece%d" % i)
-        for t in range(1, PACK):
-            product_2(t, 0, H, "bank%d" % t)
+            product_2(0, a, b, "h_piece%d" % i)
+        for t, name in ((1, "h_bank1"), (2, "h_bank2"), (3, "y_bank0")):
+            product_2(t, 0, H, name)
 
         out_rows = out_0.rearrange("(p t) c -> p t c", t=PACK)
         out_words = out_1[0].rearrange("p n t -> p (n t)").bitcast(I32)
@@ -216,8 +235,10 @@ def tile_picked_toksendggap_none_po_kernel(
                     nc.vector.tensor_tensor(res[:, t, :], h[t][:].indirect(n3_t[:, cols]), less[:, t, :], ALU.subtract)
                     nc.sync.dma_start(out_rows[:, t, a:b], res[:, t, :])
             grouped = tile([P, b - a, PACK], BF16, "o_g%d" % i)
-            last = i == len(HALVES) - 1
-            interleave(nc.vector.tensor_copy if last else nc.scalar.copy, grouped[:], res[:])
+            split = LAST_ON_VECTOR if i == len(HALVES) - 1 else 0
+            if split:
+                interleave(nc.vector.tensor_copy, grouped[:, 0:split, :], res[:, :, 0:split])
+            interleave(nc.scalar.copy, grouped[:, split:, :], res[:, :, split:])
             nc.vector.quantize_mx(
                 out=o_q[:, a:b].bitcast(FP8X4), scales=o_s[:, a:b], in_=grouped[:].rearrange("p c t -> p (c t)")
             )

@@ -20,9 +20,8 @@ P = 128
 PACK = 4
 LIST = 16
 HALF = H // 2
-WA_PIECES = [(0, 256), (256, 384), (384, 512)]
+WA_SPLIT = 128
 HALVES = [(0, HALF), (HALF, H)]
-LAST_ON_VECTOR = 160
 
 
 def interleave(engine_copy, dst, src):
@@ -53,115 +52,123 @@ def tile_picked_toksendggap_none_po_kernel(
                 queue.dma_start(dst[32 * q : 32 * q + 4, :].bitcast(I32), src[0, 4 * q : 4 * q + 4, :].bitcast(I32))
 
         xs = tile([P, T], U8, "xs")
-        w1s = tile([P, N], U8, "w1s")
-        nc.gpsimd.memset(xs[:].bitcast(I32), 0)
-        warm = tile([P, 2], F32, "warm")
+        nc.vector.memset(xs[:].bitcast(I32), 0)
+        warm = tile([P, 2], F32, "wa_raw")
         nc.vector.memset(warm[:, 0:1], 0.0)
-        nc.vector.memset(w1s[:].bitcast(I32), 0)
+        nc.scalar.activation(warm[:, 1:2], warm[:, 0:1], ACT.Sigmoid)
 
-        wa_rows = wa.rearrange("(p j) c -> p j c", j=PACK)
+        def window(name, engine):
+            rows = tile([P, 2 * H], F32, name)
+            engine.memset(rows[:, H:], 0.0)
+            return rows
 
-        def load_wa(i):
-            a, b = WA_PIECES[i]
-            raw = tile([P, PACK, b - a], F32, "wa_raw%d" % i)
-            nc.sync.dma_start(raw[:], wa_rows[:, :, a:b])
-            return raw
+        y = [window("y%d" % t, nc.vector) for t in range(PACK)]
+        h = [window("h%d" % t, nc.gpsimd) for t in range(PACK)]
 
-        load_scale_rows(nc.gpsimd, xs, x_scales)
+        offs_t = load_list(offs, "offs_t")
+        n2_t = load_list(n2, "n2_t")
+        n1_t = load_list(n1, "n1_t")
+        n4_t = load_list(n4, "n4_t")
         xw = tile([P, T], I32, "xw")
         nc.sync.dma_start(xw[:], x_words[0].rearrange("p n t -> p (n t)").bitcast(I32))
-        offs_t = load_list(offs, "offs_t")
-        nc.scalar.activation(warm[:, 1:2], warm[:, 0:1], ACT.Sigmoid)
-        wa_raw = [load_wa(i) for i in range(len(WA_PIECES))]
-        n2_t = load_list(n2, "n2_t")
-        gt_t = tile([P, PACK], F32, "gt_t")
-        nc.sync.dma_start(gt_t[:], gt.rearrange("(p t) o -> p (t o)", t=PACK))
-        n1_t = load_list(n1, "n1_t")
-        w1w = tile([P, 2 * N], U8, "w1w")
-        nc.sync.dma_start(w1w[:].bitcast(I32), w1_words[0].bitcast(I32))
-        load_scale_rows(nc.sync, w1s, w1_scales)
-        n4_t = load_list(n4, "n4_t")
         n3_t = load_list(n3, "n3_t")
+        load_scale_rows(nc.sync, xs, x_scales)
+        wa_raw = tile([P, 2, PACK, HALF], F32, "wa_raw")
+        wa_rows = wa.rearrange("(p j) c -> p j c", j=PACK)
+        for i, (a, b) in enumerate(HALVES):
+            nc.sync.dma_start(wa_raw[:, i, :, :], wa_rows[:, :, a:b])
 
-        xw_d = tile([P, S], U32, "xw_d")
-        nc.vector.tensor_copy(
-            xw_d[:].rearrange("p (t m) -> p m t", t=PACK), xw[:].bitcast(U32).indirect(offs_t[:])
-        )
+        xw_g = tile([P, S], U32, "xw_g")
+        nc.vector.tensor_copy(xw_g[:], xw[:].bitcast(U32).indirect(offs_t[:]))
+
+        def deal(src, t0, t1, dtype, name):
+            dst = tile([P, t1 - t0, P], dtype, name)
+            nc.vector.tensor_copy(dst[:].rearrange("p t m -> p m t"), src.rearrange("p (m t) -> p m t", t=PACK)[:, :, t0:t1])
+            return [dst[:, t - t0, :] for t in range(t0, t1)]
+
         xs_g = tile([P, S], U8, "xs_g")
         nc.vector.tensor_copy(xs_g[:], xs[:].indirect(offs_t[:]))
-        xs_d = tile([P, S], U8, "xs_d")
 
-        def deal_scales(t0, t1):
-            nc.vector.tensor_copy(
-                xs_d[:].rearrange("p (t m) -> p t m", t=PACK)[:, t0:t1, :],
-                xs_g[:].rearrange("p (m t) -> p t m", t=PACK)[:, t0:t1, :],
-            )
+        xw_d = deal(xw_g[:].bitcast(I32), 0, 1, I32, "xw_first")
+        xs_d = deal(xs_g[:], 0, 1, U8, "xs_first")
 
-        deal_scales(0, 1)
+        wa_g = [tile([P, HALF, PACK], BF16, "wa_g%d" % i) for i in range(2)]
+        interleave(nc.scalar.copy, wa_g[0][:], wa_raw[:, 0, :, :])
+        interleave(nc.scalar.copy, wa_g[1][:, 0:WA_SPLIT, :], wa_raw[:, 1, :, 0:WA_SPLIT])
+        interleave(nc.vector.tensor_copy, wa_g[1][:, WA_SPLIT:, :], wa_raw[:, 1, :, WA_SPLIT:])
 
         wa_q = tile([P, H], U32, "wa_q")
         wa_s = tile([P, H], U8, "wa_s")
-        y = [tile([P, H], F32, "y%d" % t) for t in range(PACK)]
 
-        y_bank = [ps.tile([P, H], F32, name="y_bank%d" % t) for t in range(PACK)]
+        def quantize_wa(i):
+            a, b = HALVES[i]
+            nc.vector.quantize_mx(
+                out=wa_q[:, a:b].bitcast(FP8X4), scales=wa_s[:, a:b], in_=wa_g[i][:].rearrange("p c t -> p (c t)")
+            )
 
-        def product_1(t, a, b):
-            m = slice(t * P, (t + 1) * P)
+        quantize_wa(0)
+        quantize_wa(1)
+        xw_d.extend(deal(xw_g[:].bitcast(I32), 1, PACK, I32, "wa_g0"))
+        xs_d.extend(deal(xs_g[:], 1, PACK, U8, "wa_g1"))
+
+        w1w = tile([P, 2 * N], U8, "wa_raw")
+        nc.sync.dma_start(w1w[:].bitcast(I32), w1_words[0].bitcast(I32))
+        w1s = tile([P, N], U8, "xs")
+        nc.gpsimd.memset(w1s[:].bitcast(I32), 0)
+        load_scale_rows(nc.sync, w1s, w1_scales)
+        gt_t = tile([P, PACK], F32, "xw")
+        nc.sync.dma_start(gt_t[:], gt.rearrange("(p t) o -> p (t o)", t=PACK))
+
+        y_bank = {}
+
+        def product_1(t, a, b, name):
+            y_bank[t, a, b] = ps.tile([P, b - a], F32, name=name)
             nc.tensor.matmul_mx(
-                out=y_bank[t][:, a:b],
-                lhsT=xw_d[:, m].bitcast(FP8X4),
-                lhsT_scale=xs_d[:, m],
+                out=y_bank[t, a, b][:],
+                lhsT=xw_d[t].bitcast(FP8X4),
+                lhsT_scale=xs_d[t],
                 rhs=wa_q[:, a:b].bitcast(FP8X4),
                 rhs_scale=wa_s[:, a:b],
                 start=True,
                 stop=True,
             )
-            nc.scalar.copy(y[t][:, a:b], y_bank[t][:, a:b])
+            nc.scalar.copy(y[t][:, a:b], y_bank[t, a, b][:])
 
-        wa_g = [tile([P, HALF, PACK], BF16, "wa_g%d" % i) for i in range(2)]
-        for i, (a, b) in enumerate(WA_PIECES):
-            last = i == len(WA_PIECES) - 1
-            dst = wa_g[a // HALF][:, a % HALF : a % HALF + b - a, :]
-            interleave(nc.vector.tensor_copy if last else nc.scalar.copy, dst, wa_raw[i][:])
         for i, (a, b) in enumerate(HALVES):
-            nc.vector.quantize_mx(
-                out=wa_q[:, a:b].bitcast(FP8X4), scales=wa_s[:, a:b], in_=wa_g[i][:].rearrange("p c t -> p (c t)")
-            )
-        deal_scales(1, PACK)
-        for a, b in HALVES:
-            product_1(0, a, b)
+            product_1(0, a, b, "piece%d" % i)
         for t in range(1, PACK):
-            product_1(t, 0, H)
+            product_1(t, 0, H, "y_bank%d" % t)
 
-        w1w_d = tile([P, 2 * N], U8, "wa_g1")
+        w1w_d = tile([P, 2 * N], U8, "w1w_d")
         nc.gpsimd.tensor_copy(
             w1w_d[:].rearrange("p (t m b) -> p t m b", t=PACK, b=2),
             w1w[:].rearrange("p (m t b) -> p t m b", t=PACK, b=2),
         )
-        w1s_d = tile([P, N], U8, "wa_g0")
+        w1s_d = tile([P, N], U8, "w1s_d")
         nc.gpsimd.tensor_copy(
             w1s_d[:].rearrange("p (t m) -> p t m", t=PACK), w1s[:].rearrange("p (m t) -> p t m", t=PACK)
         )
 
-        sig = [tile([P, H], F32, "sig%d" % t) for t in range(PACK)]
+        sig_rows = tile([P, PACK, H], F32, "wa_g1")
+        sig = [sig_rows[:, t, :] for t in range(PACK)]
         gate = [tile([P, H], F32, "gate%d" % t) for t in range(PACK - 1)]
         for t in range(PACK):
-            nc.scalar.activation(sig[t][:], y[t][:], ACT.Sigmoid)
+            nc.scalar.activation(sig[t], y[t][:, 0:H], ACT.Sigmoid)
             if t < PACK - 1:
-                nc.scalar.activation(gate[t][:], sig[t][:], ACT.Copy, scale=gt_t[:, t : t + 1])
+                nc.scalar.activation(gate[t][:], sig[t], ACT.Copy, scale=gt_t[:, t : t + 1])
 
         fetched = [tile([P, H], F32, "fetched%d" % t) for t in range(PACK)]
         sm = [tile([P, H], F32, "sm%d" % t) for t in range(PACK)]
         ds = [tile([P, 2 * H], F32, "ds%d" % t) for t in range(PACK)]
-        z_rows = tile([P, PACK - 1, H], BF16, "z_rows")
+        z_rows = tile([P, PACK, H], BF16, "z_rows")
         z_g = tile([P, H, PACK], BF16, "z_g")
 
         def fetch(t):
-            for a, b in HALVES:
-                nc.vector.tensor_copy(fetched[t][:, a:b], y[t][:].indirect(n2_t[:, a // LIST : b // LIST]))
+            nc.vector.tensor_copy(fetched[t][:], y[t][:].indirect(n2_t[:]))
 
         def larger(t):
-            nc.vector.tensor_tensor(sm[t][:], y_bank[t][:], fetched[t][:], ALU.max)
+            for a, b in HALVES if t == 0 else [(0, H)]:
+                nc.vector.tensor_tensor(sm[t][:, a:b], y_bank[t, a, b][:], fetched[t][:, a:b], ALU.max)
 
         def send(t):
             nc.vector.tensor_copy(ds[t][:].indirect(n1_t[:]), sm[t][:])
@@ -186,16 +193,15 @@ def tile_picked_toksendggap_none_po_kernel(
         weigh_aside(1, 0, H)
         nc.scalar.copy(z_g[:, :, 0:2], z_rows[:, 0:2, :].rearrange("p t c -> p c t"))
         send(2)
-        for a, b in HALVES:
-            weigh_aside(2, a, b)
-            nc.scalar.copy(z_g[:, a:b, 2:4], z_rows[:, 2, a:b].unsqueeze(2).to_broadcast([P, b - a, 2]))
+        weigh_aside(2, 0, H)
         send(3)
         for a, b in HALVES:
-            weigh(3, z_g[:, a:b, 3], a, b)
+            weigh(3, z_rows[:, 3, a:b], a, b)
+        for a, b in HALVES:
+            nc.vector.tensor_copy(z_g[:, a:b, 2:4], z_rows[:, 2:4, a:b].rearrange("p t c -> p c t"))
 
         z_q = tile([P, H], U32, "z_q")
         z_s = tile([P, H], U8, "z_s")
-        h = [tile([P, H], F32, "h%d" % t) for t in range(PACK)]
 
         def product_2(t, a, b, name):
             acc = ps.tile([P, b - a], F32, name=name)
@@ -215,34 +221,48 @@ def tile_picked_toksendggap_none_po_kernel(
                 out=z_q[:, a:b].bitcast(FP8X4), scales=z_s[:, a:b], in_=z_g[:, a:b, :].rearrange("p c t -> p (c t)")
             )
         for i, (a, b) in enumerate(HALVES):
-            product_2(0, a, b, "h_piece%d" % i)
-        for t, name in ((1, "h_bank1"), (2, "h_bank2"), (3, "y_bank0")):
-            product_2(t, 0, H, name)
+            product_2(0, a, b, "piece%d" % i)
+        for t in range(1, PACK):
+            product_2(t, 0, H, "h_bank%d" % t)
 
         out_rows = out_0.rearrange("(p t) c -> p t c", t=PACK)
         out_words = out_1[0].rearrange("p n t -> p (n t)").bitcast(I32)
         o_q = tile([P, H], I32, "o_q")
         o_s = tile([P, H], U8, "o_s")
-        for i, (a, b) in enumerate(HALVES):
-            cols = slice(a // LIST, b // LIST)
-            res = tile([P, PACK, b - a], F32, "res%d" % i)
-            less = tile([P, PACK, b - a], F32, "less%d" % i)
-            for step in range(PACK + 1):
-                if step < PACK:
-                    nc.vector.tensor_copy(less[:, step, :], h[step][:].indirect(n4_t[:, cols]))
-                if step > 0:
-                    t = step - 1
-                    nc.vector.tensor_tensor(res[:, t, :], h[t][:].indirect(n3_t[:, cols]), less[:, t, :], ALU.subtract)
-                    nc.sync.dma_start(out_rows[:, t, a:b], res[:, t, :])
-            grouped = tile([P, b - a, PACK], BF16, "o_g%d" % i)
-            split = LAST_ON_VECTOR if i == len(HALVES) - 1 else 0
-            if split:
-                interleave(nc.vector.tensor_copy, grouped[:, 0:split, :], res[:, :, 0:split])
-            interleave(nc.scalar.copy, grouped[:, split:, :], res[:, :, split:])
+        less = [tile([P, H], F32, "less%d" % t) for t in range(PACK)]
+        res = [tile([P, PACK, HALF], F32, "res%d" % i) for i in range(2)]
+        o_g = [tile([P, HALF, PACK], BF16, "o_g%d" % i) for i in range(2)]
+
+        def fetch_less(t):
+            nc.vector.tensor_copy(less[t][:], h[t][:].indirect(n4_t[:]))
+
+        def difference(i, t):
+            a, b = HALVES[i]
+            nc.vector.tensor_tensor(
+                res[i][:, t, :], h[t][:].indirect(n3_t[:, a // LIST : b // LIST]), less[t][:, a:b], ALU.subtract
+            )
+            nc.sync.dma_start(out_rows[:, t, a:b], res[i][:, t, :])
+
+        def quantize_out(i):
+            a, b = HALVES[i]
             nc.vector.quantize_mx(
-                out=o_q[:, a:b].bitcast(FP8X4), scales=o_s[:, a:b], in_=grouped[:].rearrange("p c t -> p (c t)")
+                out=o_q[:, a:b].bitcast(FP8X4), scales=o_s[:, a:b], in_=o_g[i][:].rearrange("p c t -> p (c t)")
             )
             nc.scalar.dma_start(out_words[:, a:b], o_q[:, a:b])
+
+        fetch_less(0)
+        for t in range(PACK):
+            if t + 1 < PACK:
+                fetch_less(t + 1)
+            difference(0, t)
+        interleave(nc.scalar.copy, o_g[0][:], res[0][:])
+        for t in range(PACK):
+            difference(1, t)
+            if t == 1:
+                nc.scalar.copy(o_g[1][:, :, 0:2], res[1][:, 0:2, :].rearrange("p t c -> p c t"))
+        quantize_out(0)
+        nc.vector.tensor_copy(o_g[1][:, :, 2:4], res[1][:, 2:4, :].rearrange("p t c -> p c t"))
+        quantize_out(1)
         for q in range(4):
             queue = nc.sync if q % 2 == 0 else nc.scalar
             queue.dma_start(out_2[0, 4 * q : 4 * q + 4, :].bitcast(I32), o_s[32 * q : 32 * q + 4, :].bitcast(I32))

@@ -20,7 +20,10 @@ P = 128
 PACK = 4
 LIST = 16
 HALF = H // 2
-WA_SPLIT = 128
+QUARTER = H // 4
+PIECES = [(0, HALF), (HALF, HALF + QUARTER), (HALF + QUARTER, H)]
+Z_SPLIT = 128
+OUT_SPLIT = 160
 HALVES = [(0, HALF), (HALF, H)]
 
 
@@ -92,26 +95,22 @@ def tile_picked_toksendggap_none_po_kernel(
         xw_d = deal(xw_g[:].bitcast(I32), 0, 1, I32, "xw_first")
         xs_d = deal(xs_g[:], 0, 1, U8, "xs_first")
 
-        wa_g = [tile([P, HALF, PACK], BF16, "wa_g%d" % i) for i in range(2)]
+        wa_g = [tile([P, b - a, PACK], BF16, "wa_g%d" % i) for i, (a, b) in enumerate(PIECES)]
         interleave(nc.scalar.copy, wa_g[0][:], wa_raw[:, 0, :, :])
-        interleave(nc.scalar.copy, wa_g[1][:, 0:WA_SPLIT, :], wa_raw[:, 1, :, 0:WA_SPLIT])
-        interleave(nc.vector.tensor_copy, wa_g[1][:, WA_SPLIT:, :], wa_raw[:, 1, :, WA_SPLIT:])
+        interleave(nc.scalar.copy, wa_g[1][:], wa_raw[:, 1, :, 0:QUARTER])
+        interleave(nc.vector.tensor_copy, wa_g[2][:], wa_raw[:, 1, :, QUARTER:])
 
         wa_q = tile([P, H], U32, "wa_q")
         wa_s = tile([P, H], U8, "wa_s")
-
-        def quantize_wa(i):
-            a, b = HALVES[i]
+        for i in (0, 2, 1):
+            a, b = PIECES[i]
             nc.vector.quantize_mx(
                 out=wa_q[:, a:b].bitcast(FP8X4), scales=wa_s[:, a:b], in_=wa_g[i][:].rearrange("p c t -> p (c t)")
             )
-
-        quantize_wa(0)
-        quantize_wa(1)
-        xw_d.extend(deal(xw_g[:].bitcast(I32), 1, PACK, I32, "wa_g0"))
+        xw_d.extend(deal(xw_g[:].bitcast(I32), 1, PACK, I32, "wa_raw"))
         xs_d.extend(deal(xs_g[:], 1, PACK, U8, "wa_g1"))
 
-        w1w = tile([P, 2 * N], U8, "wa_raw")
+        w1w = tile([P, 2 * N], U8, "wa_g0")
         nc.sync.dma_start(w1w[:].bitcast(I32), w1_words[0].bitcast(I32))
         w1s = tile([P, N], U8, "xs")
         nc.gpsimd.memset(w1s[:].bitcast(I32), 0)
@@ -134,8 +133,8 @@ def tile_picked_toksendggap_none_po_kernel(
             )
             nc.scalar.copy(y[t][:, a:b], y_bank[t, a, b][:])
 
-        for i, (a, b) in enumerate(HALVES):
-            product_1(0, a, b, "piece%d" % i)
+        for i in (0, 2, 1):
+            product_1(0, PIECES[i][0], PIECES[i][1], "piece%d" % i)
         for t in range(1, PACK):
             product_1(t, 0, H, "y_bank%d" % t)
 
@@ -167,7 +166,7 @@ def tile_picked_toksendggap_none_po_kernel(
             nc.vector.tensor_copy(fetched[t][:], y[t][:].indirect(n2_t[:]))
 
         def larger(t):
-            for a, b in HALVES if t == 0 else [(0, H)]:
+            for a, b in PIECES if t == 0 else [(0, H)]:
                 nc.vector.tensor_tensor(sm[t][:, a:b], y_bank[t, a, b][:], fetched[t][:, a:b], ALU.max)
 
         def send(t):
@@ -197,7 +196,8 @@ def tile_picked_toksendggap_none_po_kernel(
         send(3)
         for a, b in HALVES:
             weigh(3, z_rows[:, 3, a:b], a, b)
-        for a, b in HALVES:
+        nc.scalar.copy(z_g[:, 0:Z_SPLIT, 2:4], z_rows[:, 2:4, 0:Z_SPLIT].rearrange("p t c -> p c t"))
+        for a, b in [(Z_SPLIT, HALF), (HALF, H)]:
             nc.vector.tensor_copy(z_g[:, a:b, 2:4], z_rows[:, 2:4, a:b].rearrange("p t c -> p c t"))
 
         z_q = tile([P, H], U32, "z_q")
@@ -216,14 +216,14 @@ def tile_picked_toksendggap_none_po_kernel(
             )
             nc.scalar.copy(h[t][:, a:b], acc[:])
 
-        for a, b in HALVES:
+        for a, b in PIECES:
             nc.vector.quantize_mx(
                 out=z_q[:, a:b].bitcast(FP8X4), scales=z_s[:, a:b], in_=z_g[:, a:b, :].rearrange("p c t -> p (c t)")
             )
-        for i, (a, b) in enumerate(HALVES):
+        for i, (a, b) in enumerate(PIECES):
             product_2(0, a, b, "piece%d" % i)
         for t in range(1, PACK):
-            product_2(t, 0, H, "h_bank%d" % t)
+            product_2(t, 0, H, "y_bank%d" % t)
 
         out_rows = out_0.rearrange("(p t) c -> p t c", t=PACK)
         out_words = out_1[0].rearrange("p n t -> p (n t)").bitcast(I32)
@@ -260,8 +260,9 @@ def tile_picked_toksendggap_none_po_kernel(
             difference(1, t)
             if t == 1:
                 nc.scalar.copy(o_g[1][:, :, 0:2], res[1][:, 0:2, :].rearrange("p t c -> p c t"))
+        nc.scalar.copy(o_g[1][:, 0:OUT_SPLIT, 2:4], res[1][:, 2:4, 0:OUT_SPLIT].rearrange("p t c -> p c t"))
         quantize_out(0)
-        nc.vector.tensor_copy(o_g[1][:, :, 2:4], res[1][:, 2:4, :].rearrange("p t c -> p c t"))
+        nc.vector.tensor_copy(o_g[1][:, OUT_SPLIT:, 2:4], res[1][:, 2:4, OUT_SPLIT:].rearrange("p t c -> p c t"))
         quantize_out(1)
         for q in range(4):
             queue = nc.sync if q % 2 == 0 else nc.scalar

from contextlib import ExitStack

import concourse.mybir as mybir

K, T, S, N, H = 512, 2048, 512, 512, 512
FLOPS = 2 * K * S * H + 2 * S * N * H

F32 = mybir.dt.float32
BF16 = mybir.dt.bfloat16
I32 = mybir.dt.int32
U32 = mybir.dt.uint32
U16 = mybir.dt.uint16
U8 = mybir.dt.uint8
FP8X4 = mybir.dt.float8_e4m3fn_x4
FP4X4 = mybir.dt.float4_e2m1fn_x4
ALU = mybir.AluOpType
ACT = mybir.ActivationFunctionType

P = 128
PACK = 4
LIST = 16
HALF = H // 2
QUARTER = H // 4
PIECES = [(0, HALF), (HALF, HALF + QUARTER), (HALF + QUARTER, H)]
Z_SPLIT = 128
OUT_SPLIT = 160
HALVES = [(0, HALF), (HALF, H)]


def interleave(engine_copy, dst, src):
    engine_copy(
        out=dst.rearrange("p (c i) t -> p c t i", i=4),
        in_=src.rearrange("p t (c i) -> p c t i", i=4),
    )


def tile_picked_toksendggap_none_po_kernel(
    tc, x_words, x_scales, wa, gt, w1_words, w1_scales, offs, n1, n2, n3, n4, out_0, out_1, out_2
):
    nc = tc.nc
    with ExitStack() as ctx:
        sb = ctx.enter_context(tc.tile_pool(name="sb", bufs=1))
        ps = ctx.enter_context(tc.psum_pool(name="ps", bufs=1))

        def tile(shape, dtype, name):
            return sb.tile(shape, dtype, name=name, align_bytes=64)

        def load_list(src, name):
            dst = tile([P, H // LIST], U16, name)
            nc.sync.dma_start(dst[:], src)
            return dst

        def load_scale_rows(queue, dst, src):
            for q in range(4):
                queue.dma_start(dst[32 * q : 32 * q + 4, :].bitcast(I32), src[0, 4 * q : 4 * q + 4, :].bitcast(I32))

        xs = tile([P, T], U8, "xs")
        nc.vector.memset(xs[:].bitcast(I32), 0)
        warm = tile([P, 2], F32, "wa_raw")
        nc.vector.memset(warm[:, 0:1], 0.0)
        nc.scalar.activation(warm[:, 1:2], warm[:, 0:1], ACT.Sigmoid)

        def window(name, engine):
            rows = tile([P, 2 * H], F32, name)
            engine.memset(rows[:, H:], 0.0)
            return rows

        y = [window("y%d" % t, nc.vector) for t in range(PACK)]
        h = [window("h%d" % t, nc.gpsimd) for t in range(PACK)]

        offs_t = load_list(offs, "offs_t")
        n2_t = load_list(n2, "n2_t")
        n1_t = load_list(n1, "n1_t")
        n4_t = load_list(n4, "n4_t")
        xw = tile([P, T], I32, "xw")
        nc.sync.dma_start(xw[:], x_words[0].rearrange("p n t -> p (n t)").bitcast(I32))
        n3_t = load_list(n3, "n3_t")
        load_scale_rows(nc.sync, xs, x_scales)
        wa_raw = tile([P, 2, PACK, HALF], F32, "wa_raw")
        wa_rows = wa.rearrange("(p j) c -> p j c", j=PACK)
        for i, (a, b) in enumerate(HALVES):
            nc.sync.dma_start(wa_raw[:, i, :, :], wa_rows[:, :, a:b])

        xw_g = tile([P, S], U32, "xw_g")
        nc.vector.tensor_copy(xw_g[:], xw[:].bitcast(U32).indirect(offs_t[:]))

        def deal(src, t0, t1, dtype, name):
            dst = tile([P, t1 - t0, P], dtype, name)
            nc.vector.tensor_copy(dst[:].rearrange("p t m -> p m t"), src.rearrange("p (m t) -> p m t", t=PACK)[:, :, t0:t1])
            return [dst[:, t - t0, :] for t in range(t0, t1)]

        xs_g = tile([P, S], U8, "xs_g")
        nc.vector.tensor_copy(xs_g[:], xs[:].indirect(offs_t[:]))

        xw_d = deal(xw_g[:].bitcast(I32), 0, 1, I32, "xw_first")
        xs_d = deal(xs_g[:], 0, 1, U8, "xs_first")

        wa_g = [tile([P, b - a, PACK], BF16, "wa_g%d" % i) for i, (a, b) in enumerate(PIECES)]
        interleave(nc.scalar.copy, wa_g[0][:], wa_raw[:, 0, :, :])
        interleave(nc.scalar.copy, wa_g[1][:], wa_raw[:, 1, :, 0:QUARTER])
        interleave(nc.vector.tensor_copy, wa_g[2][:], wa_raw[:, 1, :, QUARTER:])

        wa_q = tile([P, H], U32, "wa_q")
        wa_s = tile([P, H], U8, "wa_s")
        for i in (0, 2, 1):
            a, b = PIECES[i]
            nc.vector.quantize_mx(
                out=wa_q[:, a:b].bitcast(FP8X4), scales=wa_s[:, a:b], in_=wa_g[i][:].rearrange("p c t -> p (c t)")
            )
        xw_d.extend(deal(xw_g[:].bitcast(I32), 1, PACK, I32, "wa_raw"))
        xs_d.extend(deal(xs_g[:], 1, PACK, U8, "wa_g1"))

        w1w = tile([P, 2 * N], U8, "wa_g0")
        nc.sync.dma_start(w1w[:].bitcast(I32), w1_words[0].bitcast(I32))
        w1s = tile([P, N], U8, "xs")
        nc.gpsimd.memset(w1s[:].bitcast(I32), 0)
        load_scale_rows(nc.sync, w1s, w1_scales)
        gt_t = tile([P, PACK], F32, "xw")
        nc.sync.dma_start(gt_t[:], gt.rearrange("(p t) o -> p (t o)", t=PACK))

        y_bank = {}

        def product_1(t, a, b, name):
            y_bank[t, a, b] = ps.tile([P, b - a], F32, name=name)
            nc.tensor.matmul_mx(
                out=y_bank[t, a, b][:],
                lhsT=xw_d[t].bitcast(FP8X4),
                lhsT_scale=xs_d[t],
                rhs=wa_q[:, a:b].bitcast(FP8X4),
                rhs_scale=wa_s[:, a:b],
                start=True,
                stop=True,
            )
            nc.scalar.copy(y[t][:, a:b], y_bank[t, a, b][:])

        for i in (0, 2, 1):
            product_1(0, PIECES[i][0], PIECES[i][1], "piece%d" % i)
        for t in range(1, PACK):
            product_1(t, 0, H, "y_bank%d" % t)

        w1w_d = tile([P, 2 * N], U8, "w1w_d")
        nc.gpsimd.tensor_copy(
            w1w_d[:].rearrange("p (t m b) -> p t m b", t=PACK, b=2),
            w1w[:].rearrange("p (m t b) -> p t m b", t=PACK, b=2),
        )
        w1s_d = tile([P, N], U8, "w1s_d")
        nc.gpsimd.tensor_copy(
            w1s_d[:].rearrange("p (t m) -> p t m", t=PACK), w1s[:].rearrange("p (m t) -> p t m", t=PACK)
        )

        sig_rows = tile([P, PACK, H], F32, "wa_g1")
        sig = [sig_rows[:, t, :] for t in range(PACK)]
        gate = [tile([P, H], F32, "gate%d" % t) for t in range(PACK - 1)]
        for t in range(PACK):
            nc.scalar.activation(sig[t], y[t][:, 0:H], ACT.Sigmoid)
            if t < PACK - 1:
                nc.scalar.activation(gate[t][:], sig[t], ACT.Copy, scale=gt_t[:, t : t + 1])

        fetched = [tile([P, H], F32, "fetched%d" % t) for t in range(PACK)]
        sm = [tile([P, H], F32, "sm%d" % t) for t in range(PACK)]
        ds = [tile([P, 2 * H], F32, "ds%d" % t) for t in range(PACK)]
        z_rows = tile([P, PACK, H], BF16, "z_rows")
        z_g = tile([P, H, PACK], BF16, "z_g")

        def fetch(t):
            nc.vector.tensor_copy(fetched[t][:], y[t][:].indirect(n2_t[:]))

        def larger(t):
            for a, b in PIECES if t == 0 else [(0, H)]:
                nc.vector.tensor_tensor(sm[t][:, a:b], y_bank[t, a, b][:], fetched[t][:, a:b], ALU.max)

        def send(t):
            nc.vector.tensor_copy(ds[t][:].indirect(n1_t[:]), sm[t][:])

        def weigh(t, dst, a, b):
            nc.vector.scalar_tensor_tensor(dst, ds[t][:, a:b], gt_t[:, t : t + 1], sig[t][:, a:b], ALU.mult, ALU.mult)

        def weigh_aside(t, a, b):
            nc.gpsimd.tensor_tensor(z_rows[:, t, a:b], ds[t][:, a:b], gate[t][:, a:b], ALU.mult)

        fetch(0)
        fetch(1)
        larger(0)
        fetch(2)
        larger(1)
        fetch(3)
        larger(2)
        send(0)
        weigh_aside(0, 0, H)
        larger(3)
        send(1)
        weigh_aside(1, 0, H)
        nc.scalar.copy(z_g[:, :, 0:2], z_rows[:, 0:2, :].rearrange("p t c -> p c t"))
        send(2)
        weigh_aside(2, 0, H)
        send(3)
        for a, b in HALVES:
            weigh(3, z_rows[:, 3, a:b], a, b)
        nc.scalar.copy(z_g[:, 0:Z_SPLIT, 2:4], z_rows[:, 2:4, 0:Z_SPLIT].rearrange("p t c -> p c t"))
        for a, b in [(Z_SPLIT, HALF), (HALF, H)]:
            nc.vector.tensor_copy(z_g[:, a:b, 2:4], z_rows[:, 2:4, a:b].rearrange("p t c -> p c t"))

        z_q = tile([P, H], U32, "z_q")
        z_s = tile([P, H], U8, "z_s")

        def product_2(t, a, b, name):
            acc = ps.tile([P, b - a], F32, name=name)
            nc.tensor.matmul_mx(
                out=acc[:],
                lhsT=w1w_d[:, 2 * t * P : 2 * (t + 1) * P].bitcast(FP4X4),
                lhsT_scale=w1s_d[:, t * P : (t + 1) * P],
                rhs=z_q[:, a:b].bitcast(FP8X4),
                rhs_scale=z_s[:, a:b],
                start=True,
                stop=True,
            )
            nc.scalar.copy(h[t][:, a:b], acc[:])

        for a, b in PIECES:
            nc.vector.quantize_mx(
                out=z_q[:, a:b].bitcast(FP8X4), scales=z_s[:, a:b], in_=z_g[:, a:b, :].rearrange("p c t -> p (c t)")
            )
        for i, (a, b) in enumerate(PIECES):
            product_2(0, a, b, "piece%d" % i)
        for t in range(1, PACK):
            product_2(t, 0, H, "y_bank%d" % t)

        out_rows = out_0.rearrange("(p t) c -> p t c", t=PACK)
        out_words = out_1[0].rearrange("p n t -> p (n t)").bitcast(I32)
        o_q = tile([P, H], I32, "o_q")
        o_s = tile([P, H], U8, "o_s")
        less = [tile([P, H], F32, "less%d" % t) for t in range(PACK)]
        res = [tile([P, PACK, HALF], F32, "res%d" % i) for i in range(2)]
        o_g = [tile([P, HALF, PACK], BF16, "o_g%d" % i) for i in range(2)]

        def fetch_less(t):
            nc.vector.tensor_copy(less[t][:], h[t][:].indirect(n4_t[:]))

        def difference(i, t):
            a, b = HALVES[i]
            nc.vector.tensor_tensor(
                res[i][:, t, :], h[t][:].indirect(n3_t[:, a // LIST : b // LIST]), less[t][:, a:b], ALU.subtract
            )
            nc.sync.dma_start(out_rows[:, t, a:b], res[i][:, t, :])

        def quantize_out(i):
            a, b = HALVES[i]
            nc.vector.quantize_mx(
                out=o_q[:, a:b].bitcast(FP8X4), scales=o_s[:, a:b], in_=o_g[i][:].rearrange("p c t -> p (c t)")
            )
            nc.scalar.dma_start(out_words[:, a:b], o_q[:, a:b])

        fetch_less(0)
        for t in range(PACK):
            if t + 1 < PACK:
                fetch_less(t + 1)
            difference(0, t)
        interleave(nc.scalar.copy, o_g[0][:], res[0][:])
        for t in range(PACK):
            difference(1, t)
            if t == 1:
                nc.scalar.copy(o_g[1][:, :, 0:2], res[1][:, 0:2, :].rearrange("p t c -> p c t"))
        nc.scalar.copy(o_g[1][:, 0:OUT_SPLIT, 2:4], res[1][:, 2:4, 0:OUT_SPLIT].rearrange("p t c -> p c t"))
        quantize_out(0)
        nc.vector.tensor_copy(o_g[1][:, OUT_SPLIT:, 2:4], res[1][:, 2:4, OUT_SPLIT:].rearrange("p t c -> p c t"))
        quantize_out(1)
        for q in range(4):
            queue = nc.sync if q % 2 == 0 else nc.scalar
            queue.dma_start(out_2[0, 4 * q : 4 * q + 4, :].bitcast(I32), o_s[32 * q : 32 * q + 4, :].bitcast(I32))
